import numpy as np, ml_dtypes
CORES = [16,32,48,64,80]
N = 5
import mx_ref
NC, G = 512, 2
C = np.float32(0.043)
BF = ml_dtypes.bfloat16
def cut(t, i, w=512):
    return t[:, w * i:w * i + w]
def tile(rs):
    return np.stack(rs, axis=2).reshape(128, -1).astype(BF)
def layer(w, X):
    out = []
    for i in range(G):
        for t in range(len(X)):
            p = mx_ref.matmul(mx_ref.quantize(cut(w, len(X) * i + t)), X[t])
            z = p if t == 0 else z + p
        out.append(z)
    return out
def act(Z):
    return [np.maximum(s * z, 0) * C for z in Z for s in (1, -1)]
def turned(R):
    return [np.concatenate([R[b][:, 128 * t:128 * t + 128].T for b in range(4)], axis=1) for t in range(4)]
def setup_inputs(rng):
    def f(*shape):
        return mx_ref.flush((rng.standard_normal(shape, dtype=np.float32) * np.exp2(rng.integers(-2, 3, shape[:-1] + (1,)))).astype(BF))
    return {"x": f(N, 128, 4 * 512), "w1": f(N, 128, G * 512), "w2": f(N, 128, 512), "e": f(N, 128, 4 * NC)}
def setup_inputs_blocks(rng):
    d = setup_inputs(rng)
    for k in ("x", "w1", "w2", "e"): d[k] = mx_ref.spread(d[k], rng, 4)
    return d
def setup_inputs_wide(rng):
    d = setup_inputs(rng)
    for k in ("x", "w1", "w2", "e"): d[k] = mx_ref.flush((d[k].astype(np.float32) * np.exp2(rng.integers(-6, 7, (N, 1, 1))).astype(np.float32)).astype(BF))
    return d
def setup_inputs_zeros(rng):
    d = setup_inputs(rng); v = d["x"].reshape(N, 128, -1, 4).copy()
    v[np.broadcast_to((rng.random((N, 1, v.shape[2], 1)) < 0.33), v.shape)] = 0
    d["x"] = v.reshape(d["x"].shape)
    return d
def reference(x, w1, w2, e):
    R = [act(layer(w1[j], [mx_ref.quantize(x[j])])) for j in range(N)]
    H = [mx_ref.quantize(tile(R[j])) for j in range(N)]
    K = [tile(turned(R[j])) for j in range(N)]
    y = np.zeros((N, 128, 512), np.float32); z = np.zeros((N, 128, 4 * NC), np.float32)
    for r in range(N):
        y[r] = mx_ref.matmul(mx_ref.quantize(w2[r]), H[(r - 1) % N]); qe = mx_ref.quantize(e[r])
        for b in range(4):
            z[r][:, NC * b:NC * b + NC] = mx_ref.matmul(mx_ref.quantize(cut(K[(r + 1) % N], b)), qe)
    return {"y": y, "z": z}

@@ -1,0 +1,207 @@
+from concourse.mybir import dt, AluOpType, ActivationFunctionType
+
+C = 0.043
+
+SCRATCH = {
+    "xb": ("sbuf", [128, 2048], "bfloat16"),
+    "wb": ("sbuf", [128, 1024], "bfloat16"),
+    "w2b": ("sbuf", [128, 512], "bfloat16"),
+    "eb": ("sbuf", [128, 2048], "bfloat16"),
+    "qx": ("sbuf", [128, 512], "float8_e4m3fn_x4"), "sx": ("sbuf", [128, 512], "uint8"),
+    "qw": ("sbuf", [128, 256], "float8_e4m3fn_x4"), "sw": ("sbuf", [128, 256], "uint8"),
+    "qv": ("sbuf", [128, 128], "float8_e4m3fn_x4"), "sv": ("sbuf", [128, 128], "uint8"),
+    "qe": ("sbuf", [128, 512], "float8_e4m3fn_x4"), "se": ("sbuf", [128, 512], "uint8"),
+    "hb": ("sbuf", [128, 2048], "bfloat16"),
+    "kb": ("sbuf", [128, 2048], "bfloat16"),
+    "qh": ("sbuf", [128, 512], "float8_e4m3fn_x4"), "sh": ("sbuf", [128, 512], "uint8"),
+    "qk": ("sbuf", [128, 512], "float8_e4m3fn_x4"), "sk": ("sbuf", [128, 512], "uint8"),
+    "rh": ("sbuf", [128, 512], "float8_e4m3fn_x4"), "rsh": ("sbuf", [128, 512], "uint8"),
+    "rk": ("sbuf", [128, 512], "float8_e4m3fn_x4"), "rsk": ("sbuf", [128, 512], "uint8"),
+    "yo": ("sbuf", [128, 512], "float32"),
+    "zo": ("sbuf", [128, 2048], "float32"),
+    "ps": ("psum", [128, 4096], "float32"),
+}
+SEMAPHORES = [
+    "l_x0", "l_xr", "l_w", "l_w2", "l_e",
+    "q_x0", "q_x1", "q_x2", "q_x3", "q_w", "q_w2", "q_e",
+    "m_h0", "m_h1", "m_h2", "m_h3", "m_k0", "m_k1", "m_k2", "m_k3",
+    "a_h0", "a_hr", "a_kp", "a_km",
+    "q_h0", "q_hr", "q_kp", "q_km",
+    "r_ka", "r_kb", "r_h", "sent",
+    "m_z0", "m_z1", "m_z2", "m_z3a", "m_z3b", "m_ya", "m_yb",
+    "c_z0", "c_z1", "c_z2", "c_z3", "c_y",
+    "st_s", "st_a",
+]
+
+
+def rank_program(g, core, T, topo):
+    rank = T.rank_of(core)
+    if rank is None:
+        return
+    n = len(T.cores)
+    S = T.sem
+    V, A, PE, SY = g.vector, g.scalar, g.tensor, g.sync
+    MULT, MAX = AluOpType.mult, AluOpType.max
+    RELU, COPY = ActivationFunctionType.Relu, ActivationFunctionType.Copy
+
+    def bank(i, w):
+        return T.ps[:, 512 * i:512 * i + w]
+
+    def act_s(out, i, w, c, sem):
+        A.activation(out, bank(i, w), RELU, bias=0.0, scale=c).then_inc(sem, 1)
+
+    def act_v(out, i, w, c, sem):
+        V.tensor_scalar(out, bank(i, w), c, 0.0, MULT, MAX).then_inc(sem, 1)
+
+    def hcols(b, lo, hi):
+        return T.hb[:, 4 * lo + b:4 * hi:4]
+
+    def kcols(s, t):
+        return T.kb[:, 1024 * s + t:1024 * s + 1024:4]
+
+    SY.dma_start(T.xb[:, 0:512], T.x[:, 0:512]).then_inc(S.l_x0, 16)
+    A.dma_start(T.wb[:], T.w1[:]).then_inc(S.l_w, 16)
+    SY.dma_start(T.xb[:, 512:2048], T.x[:, 512:2048]).then_inc(S.l_xr, 16)
+    SY.dma_start(T.eb[:], T.e[:]).then_inc(S.l_e, 16)
+    SY.dma_start(T.w2b[:], T.w2[:]).then_inc(S.l_w2, 16)
+
+    def w1(i):
+        return T.qw[:, 128 * i:128 * i + 128], T.sw[:, 128 * i:128 * i + 128]
+
+    def xs(lo, hi):
+        return T.qx[:, lo:hi], T.sx[:, lo:hi]
+
+    def mm(out, w, x, sem):
+        PE.matmul_mx(out, w[0], w[1], x[0], x[1], True, True).then_inc(sem, 1)
+
+    allw = (T.qw[:, 0:256], T.sw[:, 0:256])
+    PE.wait_ge(S.q_x0, 1)
+    PE.wait_ge(S.q_w, 1)
+    mm(bank(0, 128), w1(0), xs(0, 128), S.m_h0)
+    mm(bank(1, 128), w1(1), xs(0, 128), S.m_h1)
+    mm(bank(4, 256), xs(0, 128), allw, S.m_k0)
+    for t in (1, 2, 3):
+        PE.wait_ge(S["q_x%d" % t], 1)
+        mm(bank(4 + t, 256), xs(128 * t, 128 * t + 128), allw, S["m_k%d" % t])
+    mm(bank(2, 384), w1(0), xs(128, 512), S.m_h2)
+    mm(bank(3, 384), w1(1), xs(128, 512), S.m_h3)
+
+    A.wait_ge(S.m_h0, 1)
+    act_s(hcols(0, 0, 128), 0, 128, C, S.a_h0)
+    act_s(hcols(1, 0, 128), 0, 128, -C, S.a_h0)
+    for t in (0, 1, 3):
+        A.wait_ge(S["m_k%d" % t], 1)
+        act_s(kcols(0, t), 4 + t, 256, C, S.a_kp)
+        act_s(kcols(1, t), 4 + t, 256, -C, S.a_km)
+    A.wait_ge(S.m_h2, 1)
+    act_s(hcols(0, 128, 512), 2, 384, C, S.a_hr)
+    act_s(hcols(1, 128, 512), 2, 384, -C, S.a_hr)
+
+    def quant(q, s, b, lo, hi, sem):
+        V.quantize_mx(q[:, lo:hi], s[:, lo:hi], b[:, 4 * lo:4 * hi]).then_inc(sem, 1)
+
+    V.wait_ge(S.l_x0, 16)
+    quant(T.qx, T.sx, T.xb, 0, 128, S.q_x0)
+    V.wait_ge(S.l_w, 16)
+    quant(T.qw, T.sw, T.wb, 0, 256, S.q_w)
+    V.wait_ge(S.m_h1, 1)
+    act_v(hcols(2, 0, 128), 1, 128, C, S.a_h0)
+    act_v(hcols(3, 0, 128), 1, 128, -C, S.a_h0)
+    V.wait_ge(S.a_h0, 4)
+    quant(T.qh, T.sh, T.hb, 0, 128, S.q_h0)
+    V.wait_ge(S.l_xr, 16)
+    for t in (1, 2, 3):
+        quant(T.qx, T.sx, T.xb, 128 * t, 128 * t + 128, S["q_x%d" % t])
+    V.wait_ge(S.m_k2, 1)
+    act_v(kcols(0, 2), 6, 256, C, S.a_kp)
+    act_v(kcols(1, 2), 6, 256, -C, S.a_km)
+    V.wait_ge(S.a_kp, 4)
+    quant(T.qk, T.sk, T.kb, 0, 256, S.q_kp)
+    V.wait_ge(S.a_km, 4)
+    quant(T.qk, T.sk, T.kb, 256, 512, S.q_km)
+    V.wait_ge(S.m_h3, 1)
+    act_v(hcols(2, 128, 512), 3, 384, C, S.a_hr)
+    act_v(hcols(3, 128, 512), 3, 384, -C, S.a_hr)
+    V.wait_ge(S.a_hr, 4)
+    quant(T.qh, T.sh, T.hb, 128, 512, S.q_hr)
+    V.wait_ge(S.l_e, 16)
+    quant(T.qe, T.se, T.eb, 0, 512, S.q_e)
+    V.wait_ge(S.l_w2, 16)
+    quant(T.qv, T.sv, T.w2b, 0, 128, S.q_w2)
+
+    def send(dst, out, src, sem):
+        rid, pid, _ = topo.addr(dst)
+        g.remote_dma(out, src, sem, S.sent, pid, rid, topo.mask(core, dst))
+        return bin(topo.mask(core, dst)).count("1")
+
+    def codes(t, lo, hi):
+        return t[:, lo:hi].bitcast(dt.uint8)
+
+    hd, kd = T.cores[(rank + 1) % n], T.cores[(rank - 1) % n]
+    out = 0
+    g.wait_ge(S.q_h0, 1)
+    out += send(hd, codes(T.rh, 0, 128), codes(T.qh, 0, 128), S.r_h)
+    g.wait_ge(S.q_kp, 1)
+    out += send(kd, codes(T.rk, 0, 256), codes(T.qk, 0, 256), S.r_ka)
+    g.wait_ge(S.q_km, 1)
+    out += send(kd, T.rsk[:, 0:512], T.sk[:, 0:512], S.r_ka)
+    out += send(kd, codes(T.rk, 256, 512), codes(T.qk, 256, 512), S.r_kb)
+    g.wait_ge(S.q_hr, 1)
+    out += send(hd, codes(T.rh, 128, 512), codes(T.qh, 128, 512), S.r_h)
+    out += send(hd, T.rsh[:, 0:512], T.sh[:, 0:512], S.r_h)
+    g.wait_ge(S.sent, out)
+
+    hs, ks = T.cores[(rank - 1) % n], T.cores[(rank + 1) % n]
+    hn, kn = bin(topo.mask(hs, core)).count("1"), bin(topo.mask(ks, core)).count("1")
+
+    def kblk(b):
+        lo = 256 * (b % 2) + 128 * (b // 2)
+        return T.rk[:, lo:lo + 128], T.rsk[:, lo:lo + 128]
+
+    def es(lo, hi):
+        return T.qe[:, lo:hi], T.se[:, lo:hi]
+
+    for name in ("a_kp", "a_km", "a_h0", "a_hr"):
+        PE.wait_ge(S[name], 4)
+    PE.wait_ge(S.q_e, 1)
+    PE.wait_ge(S.r_ka, 2 * kn)
+    mm(bank(4, 512), kblk(0), es(0, 512), S.m_z0)
+    mm(bank(5, 512), kblk(2), es(0, 512), S.m_z2)
+    PE.wait_ge(S.r_kb, kn)
+    mm(bank(6, 512), kblk(1), es(0, 512), S.m_z1)
+    mm(bank(7, 256), kblk(3), es(0, 256), S.m_z3a)
+    mm(bank(0, 256), kblk(3), es(256, 512), S.m_z3b)
+    PE.wait_ge(S.q_w2, 1)
+    PE.wait_ge(S.r_h, 3 * hn)
+    v = (T.qv[:, 0:128], T.sv[:, 0:128])
+    mm(bank(1, 256), v, (T.rh[:, 0:256], T.rsh[:, 0:256]), S.m_ya)
+    mm(bank(2, 256), v, (T.rh[:, 256:512], T.rsh[:, 256:512]), S.m_yb)
+
+    def copy_v(dst, i, w, done, sem):
+        V.wait_ge(done, 1)
+        V.tensor_copy(dst, bank(i, w)).then_inc(sem, 1)
+
+    def copy_s(dst, i, w, done, sem):
+        A.wait_ge(done, 1)
+        A.activation(dst, bank(i, w), COPY).then_inc(sem, 1)
+
+    copy_v(T.zo[:, 0:512], 4, 512, S.m_z0, S.c_z0)
+    copy_s(T.zo[:, 1024:1536], 5, 512, S.m_z2, S.c_z2)
+    copy_v(T.zo[:, 512:1024], 6, 512, S.m_z1, S.c_z1)
+    copy_s(T.zo[:, 1536:1792], 7, 256, S.m_z3a, S.c_z3)
+    copy_v(T.zo[:, 1792:2048], 0, 256, S.m_z3b, S.c_z3)
+    A.wait_ge(S.c_z3, 2)
+    A.dma_start(T.z[:, 1536:2048], T.zo[:, 1536:2048]).then_inc(S.st_a, 16)
+    copy_s(T.yo[:, 0:256], 1, 256, S.m_ya, S.c_y)
+    copy_v(T.yo[:, 256:512], 2, 256, S.m_yb, S.c_y)
+    A.wait_ge(S.st_a, 16)
+
+    SY.wait_ge(S.c_z0, 1)
+    SY.dma_start(T.z[:, 0:512], T.zo[:, 0:512]).then_inc(S.st_s, 16)
+    SY.wait_ge(S.c_z2, 1)
+    SY.dma_start(T.z[:, 1024:1536], T.zo[:, 1024:1536]).then_inc(S.st_s, 16)
+    SY.wait_ge(S.c_z1, 1)
+    SY.dma_start(T.z[:, 512:1024], T.zo[:, 512:1024]).then_inc(S.st_s, 16)
+    SY.wait_ge(S.c_y, 2)
+    SY.dma_start(T.y[:], T.yo[:]).then_inc(S.st_s, 16)
+    SY.wait_ge(S.st_s, 64)

@@ -1,48 +1,52 @@
 from concourse.mybir import dt, AluOpType, ActivationFunctionType
 
 C = 0.043
+CORES_SIMULATED = 96
+XP = [(0, 128), (128, 384), (384, 512)]
+HT = 320
+PIECES = [(0, 128), (128, HT)]
 
-SCRATCH = {
-    "xb": ("sbuf", [128, 2048], "bfloat16"),
-    "wb": ("sbuf", [128, 1024], "bfloat16"),
-    "w2b": ("sbuf", [128, 512], "bfloat16"),
-    "eb": ("sbuf", [128, 2048], "bfloat16"),
-    "qx": ("sbuf", [128, 512], "float8_e4m3fn_x4"), "sx": ("sbuf", [128, 512], "uint8"),
-    "qw": ("sbuf", [128, 256], "float8_e4m3fn_x4"), "sw": ("sbuf", [128, 256], "uint8"),
-    "qv": ("sbuf", [128, 128], "float8_e4m3fn_x4"), "sv": ("sbuf", [128, 128], "uint8"),
-    "qe": ("sbuf", [128, 512], "float8_e4m3fn_x4"), "se": ("sbuf", [128, 512], "uint8"),
-    "hb": ("sbuf", [128, 2048], "bfloat16"),
-    "kb": ("sbuf", [128, 2048], "bfloat16"),
-    "qh": ("sbuf", [128, 512], "float8_e4m3fn_x4"), "sh": ("sbuf", [128, 512], "uint8"),
-    "qk": ("sbuf", [128, 512], "float8_e4m3fn_x4"), "sk": ("sbuf", [128, 512], "uint8"),
-    "rh": ("sbuf", [128, 512], "float8_e4m3fn_x4"), "rsh": ("sbuf", [128, 512], "uint8"),
-    "rk": ("sbuf", [128, 512], "float8_e4m3fn_x4"), "rsk": ("sbuf", [128, 512], "uint8"),
-    "yo": ("sbuf", [128, 512], "float32"),
-    "zo": ("sbuf", [128, 2048], "float32"),
-    "ps": ("psum", [128, 4096], "float32"),
-}
-SEMAPHORES = [
-    "l_x0", "l_xr", "l_w", "l_w2", "l_e",
-    "q_x0", "q_x1", "q_x2", "q_x3", "q_w", "q_w2", "q_e",
-    "m_h0", "m_h1", "m_h2", "m_h3", "m_k0", "m_k1", "m_k2", "m_k3",
-    "a_h0", "a_hr", "a_kp", "a_km",
-    "q_h0", "q_hr", "q_kp", "q_km",
-    "r_ka", "r_kb", "r_h", "sent",
-    "m_z0", "m_z1", "m_z2", "m_z3a", "m_z3b", "m_ya", "m_yb",
-    "c_z0", "c_z1", "c_z2", "c_z3", "c_y",
-    "st_s", "st_a",
-]
+Q, U, B, F = "float8_e4m3fn_x4", "uint8", "bfloat16", "float32"
+SCRATCH = {"ps": ("psum", [128, 4096], F)}
+for _name, _cols, _dtype in (
+        ("xb", 2048, B), ("wb", 1024, B), ("w2b", 512, B), ("eb", 2048, B),
+        ("qx", 512, Q), ("sx", 512, U), ("qw", 256, Q), ("sw", 256, U),
+        ("qv", 128, Q), ("sv", 128, U), ("qe", 512, Q), ("se", 512, U),
+        ("kb", 2048, B), ("qk", 512, Q), ("sk", 512, U),
+        ("hb", 2048, B), ("qh", 512, Q), ("sh", 512, U),
+        ("rk", 512, Q), ("rsk", 512, U), ("rh", 512, Q), ("rsh", 512, U),
+        ("yo", 512, F), ("zo", 2048, F)):
+    SCRATCH[_name] = ("sbuf", [128, _cols], _dtype)
+SEMAPHORES = (
+    "l_x0 l_x1 l_x2 l_w l_w2 l_e q_x0 q_x1 q_x2 q_x3 q_w q_w2 q_e "
+    "m_k0 m_k1 m_k2 m_k3 a_kp a_km q_kp q_km "
+    "m_ra m_rb a_hr q_hr "
+    "r_w r_x m_a0 m_a1 m_b0 m_b1 a_h0 a_h1 q_h0 q_h1 "
+    "sent r_ka r_k1 r_k3 r_hh r_hr "
+    "m_z0a m_z0b m_z1a m_z1b m_z2a m_z2b m_z3a m_z3b m_ya m_yb "
+    "c_z0 c_z1 c_z2 c_z3 c_y st_s st_a").split()
+
+
+def engines(mask):
+    return bin(mask).count("1")
 
 
 def rank_program(g, core, T, topo):
-    rank = T.rank_of(core)
-    if rank is None:
-        return
     n = len(T.cores)
     S = T.sem
     V, A, PE, SY = g.vector, g.scalar, g.tensor, g.sync
     MULT, MAX = AluOpType.mult, AluOpType.max
     RELU, COPY = ActivationFunctionType.Relu, ActivationFunctionType.Copy
+
+    def helper_of(r):
+        c = T.cores[r]
+        return [d for d in range(CORES_SIMULATED) if topo.chip(d) == topo.chip(c) and topo.die(d) != topo.die(c)
+                and topo.may_write(d, T.cores[(r + 1) % n])][0]
+
+    helpers = [helper_of(r) for r in range(n)]
+    rank = T.rank_of(core)
+    if rank is None and core not in helpers:
+        return
 
     def bank(i, w):
         return T.ps[:, 512 * i:512 * i + w]
@@ -53,129 +57,164 @@ def rank_program(g, core, T, topo):
     def act_v(out, i, w, c, sem):
         V.tensor_scalar(out, bank(i, w), c, 0.0, MULT, MAX).then_inc(sem, 1)
 
-    def hcols(b, lo, hi):
-        return T.hb[:, 4 * lo + b:4 * hi:4]
-
-    def kcols(s, t):
-        return T.kb[:, 1024 * s + t:1024 * s + 1024:4]
-
-    SY.dma_start(T.xb[:, 0:512], T.x[:, 0:512]).then_inc(S.l_x0, 16)
-    A.dma_start(T.wb[:], T.w1[:]).then_inc(S.l_w, 16)
-    SY.dma_start(T.xb[:, 512:2048], T.x[:, 512:2048]).then_inc(S.l_xr, 16)
-    SY.dma_start(T.eb[:], T.e[:]).then_inc(S.l_e, 16)
-    SY.dma_start(T.w2b[:], T.w2[:]).then_inc(S.l_w2, 16)
-
-    def w1(i):
-        return T.qw[:, 128 * i:128 * i + 128], T.sw[:, 128 * i:128 * i + 128]
-
-    def xs(lo, hi):
-        return T.qx[:, lo:hi], T.sx[:, lo:hi]
+    def quant(q, s, b, lo, hi, sem):
+        V.quantize_mx(q[:, lo:hi], s[:, lo:hi], b[:, 4 * lo:4 * hi]).then_inc(sem, 1)
 
     def mm(out, w, x, sem):
         PE.matmul_mx(out, w[0], w[1], x[0], x[1], True, True).then_inc(sem, 1)
 
-    allw = (T.qw[:, 0:256], T.sw[:, 0:256])
-    PE.wait_ge(S.q_x0, 1)
-    PE.wait_ge(S.q_w, 1)
-    mm(bank(0, 128), w1(0), xs(0, 128), S.m_h0)
-    mm(bank(1, 128), w1(1), xs(0, 128), S.m_h1)
-    mm(bank(4, 256), xs(0, 128), allw, S.m_k0)
-    for t in (1, 2, 3):
-        PE.wait_ge(S["q_x%d" % t], 1)
-        mm(bank(4 + t, 256), xs(128 * t, 128 * t + 128), allw, S["m_k%d" % t])
-    mm(bank(2, 384), w1(0), xs(128, 512), S.m_h2)
-    mm(bank(3, 384), w1(1), xs(128, 512), S.m_h3)
+    def pair(q, s, lo, hi):
+        return q[:, lo:hi], s[:, lo:hi]
 
-    A.wait_ge(S.m_h0, 1)
-    act_s(hcols(0, 0, 128), 0, 128, C, S.a_h0)
-    act_s(hcols(1, 0, 128), 0, 128, -C, S.a_h0)
+    def write(dst, out, src, sem):
+        rid, pid, _ = topo.addr(dst)
+        g.remote_dma(out, src, sem, S.sent, pid, rid, topo.mask(core, dst))
+        return engines(topo.mask(core, dst))
+
+    def put_codes(dst, out, src, lo, hi, sem):
+        return write(dst, out[:, lo:hi].bitcast(dt.uint8), src[:, lo:hi].bitcast(dt.uint8), sem)
+
+    def put_plane(dst, out, src, lo, hi, sem):
+        return write(dst, out[:, lo:hi], src[:, lo:hi], sem)
+
+    def hcols(b, lo, hi):
+        return T.hb[:, 4 * lo + b:4 * hi:4]
+
+    if rank is None:
+        r = helpers.index(core)
+        dst = T.cores[(r + 1) % n]
+        on = engines(topo.mask(T.cores[r], core))
+        PE.wait_ge(S.r_w, 4 * on)
+        out = 0
+        for i, (lo, hi) in enumerate(PIECES):
+            if i == 1:
+                PE.wait_ge(S.r_x, 2 * on)
+            mm(bank(2 * i, hi - lo), pair(T.qw, T.sw, 0, 128), pair(T.qx, T.sx, lo, hi), S["m_a%d" % i])
+            mm(bank(2 * i + 1, hi - lo), pair(T.qw, T.sw, 128, 256), pair(T.qx, T.sx, lo, hi), S["m_b%d" % i])
+            done = S["a_h%d" % i]
+            A.wait_ge(S["m_a%d" % i], 1)
+            act_s(hcols(0, lo, hi), 2 * i, hi - lo, C, done)
+            act_s(hcols(1, lo, hi), 2 * i, hi - lo, -C, done)
+            V.wait_ge(S["m_b%d" % i], 1)
+            act_v(hcols(2, lo, hi), 2 * i + 1, hi - lo, C, done)
+            act_v(hcols(3, lo, hi), 2 * i + 1, hi - lo, -C, done)
+            V.wait_ge(done, 4)
+            quant(T.qh, T.sh, T.hb, lo, hi, S["q_h%d" % i])
+            g.wait_ge(S["q_h%d" % i], 1)
+            if i == 1:
+                out += put_plane(dst, T.rsh, T.sh, 0, HT, S.r_hh)
+            out += put_codes(dst, T.rh, T.qh, lo, hi, S.r_hh)
+        g.wait_ge(S.sent, out)
+        return
+
+    helper, prev, nxt = helpers[rank], T.cores[(rank - 1) % n], T.cores[(rank + 1) % n]
+
+    def kcols(s, t):
+        return T.kb[:, 1024 * s + t:1024 * s + 1024:4]
+
+    def load_x(i):
+        lo, hi = XP[i]
+        SY.dma_start(T.xb[:, 4 * lo:4 * hi], T.x[:, 4 * lo:4 * hi]).then_inc(S["l_x%d" % i], 16)
+
+    load_x(0)
+    SY.dma_start(T.wb[:], T.w1[:]).then_inc(S.l_w, 16)
+    load_x(1)
+    load_x(2)
+    SY.dma_start(T.eb[:], T.e[:]).then_inc(S.l_e, 16)
+    SY.wait_ge(S.q_kp, 1)
+    SY.dma_start(T.w2b[:], T.w2[:]).then_inc(S.l_w2, 16)
+
+    PE.wait_ge(S.q_w, 1)
+    for t in range(4):
+        PE.wait_ge(S["q_x%d" % t], 1)
+        mm(bank(t, 256), pair(T.qx, T.sx, 128 * t, 128 * t + 128), pair(T.qw, T.sw, 0, 256), S["m_k%d" % t])
+    mm(bank(4, 512 - HT), pair(T.qw, T.sw, 0, 128), pair(T.qx, T.sx, HT, 512), S.m_ra)
+    mm(bank(5, 512 - HT), pair(T.qw, T.sw, 128, 256), pair(T.qx, T.sx, HT, 512), S.m_rb)
+
     for t in (0, 1, 3):
         A.wait_ge(S["m_k%d" % t], 1)
-        act_s(kcols(0, t), 4 + t, 256, C, S.a_kp)
-        act_s(kcols(1, t), 4 + t, 256, -C, S.a_km)
-    A.wait_ge(S.m_h2, 1)
-    act_s(hcols(0, 128, 512), 2, 384, C, S.a_hr)
-    act_s(hcols(1, 128, 512), 2, 384, -C, S.a_hr)
-
-    def quant(q, s, b, lo, hi, sem):
-        V.quantize_mx(q[:, lo:hi], s[:, lo:hi], b[:, 4 * lo:4 * hi]).then_inc(sem, 1)
+        act_s(kcols(0, t), t, 256, C, S.a_kp)
+    for t in (0, 1, 3):
+        act_s(kcols(1, t), t, 256, -C, S.a_km)
+    A.wait_ge(S.m_ra, 1)
+    act_s(hcols(0, HT, 512), 4, 512 - HT, C, S.a_hr)
+    act_s(hcols(1, HT, 512), 4, 512 - HT, -C, S.a_hr)
 
     V.wait_ge(S.l_x0, 16)
     quant(T.qx, T.sx, T.xb, 0, 128, S.q_x0)
     V.wait_ge(S.l_w, 16)
     quant(T.qw, T.sw, T.wb, 0, 256, S.q_w)
-    V.wait_ge(S.m_h1, 1)
-    act_v(hcols(2, 0, 128), 1, 128, C, S.a_h0)
-    act_v(hcols(3, 0, 128), 1, 128, -C, S.a_h0)
-    V.wait_ge(S.a_h0, 4)
-    quant(T.qh, T.sh, T.hb, 0, 128, S.q_h0)
-    V.wait_ge(S.l_xr, 16)
-    for t in (1, 2, 3):
-        quant(T.qx, T.sx, T.xb, 128 * t, 128 * t + 128, S["q_x%d" % t])
+    V.wait_ge(S.l_x1, 16)
+    quant(T.qx, T.sx, T.xb, 128, 256, S.q_x1)
+    quant(T.qx, T.sx, T.xb, 256, 384, S.q_x2)
+    V.wait_ge(S.l_x2, 16)
+    quant(T.qx, T.sx, T.xb, 384, 512, S.q_x3)
     V.wait_ge(S.m_k2, 1)
-    act_v(kcols(0, 2), 6, 256, C, S.a_kp)
-    act_v(kcols(1, 2), 6, 256, -C, S.a_km)
+    act_v(kcols(0, 2), 2, 256, C, S.a_kp)
     V.wait_ge(S.a_kp, 4)
     quant(T.qk, T.sk, T.kb, 0, 256, S.q_kp)
+    act_v(kcols(1, 2), 2, 256, -C, S.a_km)
     V.wait_ge(S.a_km, 4)
     quant(T.qk, T.sk, T.kb, 256, 512, S.q_km)
-    V.wait_ge(S.m_h3, 1)
-    act_v(hcols(2, 128, 512), 3, 384, C, S.a_hr)
-    act_v(hcols(3, 128, 512), 3, 384, -C, S.a_hr)
+    V.wait_ge(S.m_rb, 1)
+    act_v(hcols(2, HT, 512), 5, 512 - HT, C, S.a_hr)
+    act_v(hcols(3, HT, 512), 5, 512 - HT, -C, S.a_hr)
     V.wait_ge(S.a_hr, 4)
-    quant(T.qh, T.sh, T.hb, 128, 512, S.q_hr)
+    quant(T.qh, T.sh, T.hb, HT, 512, S.q_hr)
     V.wait_ge(S.l_e, 16)
     quant(T.qe, T.se, T.eb, 0, 512, S.q_e)
     V.wait_ge(S.l_w2, 16)
     quant(T.qv, T.sv, T.w2b, 0, 128, S.q_w2)
 
-    def send(dst, out, src, sem):
-        rid, pid, _ = topo.addr(dst)
-        g.remote_dma(out, src, sem, S.sent, pid, rid, topo.mask(core, dst))
-        return bin(topo.mask(core, dst)).count("1")
-
-    def codes(t, lo, hi):
-        return t[:, lo:hi].bitcast(dt.uint8)
-
-    hd, kd = T.cores[(rank + 1) % n], T.cores[(rank - 1) % n]
-    out = 0
-    g.wait_ge(S.q_h0, 1)
-    out += send(hd, codes(T.rh, 0, 128), codes(T.qh, 0, 128), S.r_h)
+    g.wait_ge(S.q_x0, 1)
+    out = put_codes(helper, T.qx, T.qx, 0, 128, S.r_w)
+    g.wait_ge(S.q_w, 1)
+    out += put_codes(helper, T.qw, T.qw, 0, 256, S.r_w)
+    out += put_plane(helper, T.sx, T.sx, 0, 128, S.r_w)
+    out += put_plane(helper, T.sw, T.sw, 0, 256, S.r_w)
+    for t in (1, 2):
+        g.wait_ge(S["q_x%d" % t], 1)
+    out += put_plane(helper, T.sx, T.sx, 128, HT, S.r_x)
+    out += put_codes(helper, T.qx, T.qx, 128, HT, S.r_x)
     g.wait_ge(S.q_kp, 1)
-    out += send(kd, codes(T.rk, 0, 256), codes(T.qk, 0, 256), S.r_ka)
+    out += put_codes(prev, T.rk, T.qk, 0, 256, S.r_ka)
+    out += put_plane(prev, T.rsk, T.sk, 0, 256, S.r_ka)
     g.wait_ge(S.q_km, 1)
-    out += send(kd, T.rsk[:, 0:512], T.sk[:, 0:512], S.r_ka)
-    out += send(kd, codes(T.rk, 256, 512), codes(T.qk, 256, 512), S.r_kb)
+    out += put_plane(prev, T.rsk, T.sk, 256, 512, S.r_k1)
+    out += put_codes(prev, T.rk, T.qk, 256, 384, S.r_k1)
+    out += put_codes(prev, T.rk, T.qk, 384, 512, S.r_k3)
     g.wait_ge(S.q_hr, 1)
-    out += send(hd, codes(T.rh, 128, 512), codes(T.qh, 128, 512), S.r_h)
-    out += send(hd, T.rsh[:, 0:512], T.sh[:, 0:512], S.r_h)
+    out += put_plane(nxt, T.rsh, T.sh, HT, 512, S.r_hr)
+    out += put_codes(nxt, T.rh, T.qh, HT, 512, S.r_hr)
     g.wait_ge(S.sent, out)
 
-    hs, ks = T.cores[(rank - 1) % n], T.cores[(rank + 1) % n]
-    hn, kn = bin(topo.mask(hs, core)).count("1"), bin(topo.mask(ks, core)).count("1")
+    kn = engines(topo.mask(nxt, core))
+    hh = engines(topo.mask(helpers[(rank - 1) % n], core))
+    hr = engines(topo.mask(prev, core))
 
-    def kblk(b):
+    def zmm(b, i, j):
         lo = 256 * (b % 2) + 128 * (b // 2)
-        return T.rk[:, lo:lo + 128], T.rsk[:, lo:lo + 128]
+        k = pair(T.rk, T.rsk, lo, lo + 128)
+        mm(bank(i, 256), k, pair(T.qe, T.se, 0, 256), S["m_z%da" % b])
+        mm(bank(j, 256), k, pair(T.qe, T.se, 256, 512), S["m_z%db" % b])
 
-    def es(lo, hi):
-        return T.qe[:, lo:hi], T.se[:, lo:hi]
-
-    for name in ("a_kp", "a_km", "a_h0", "a_hr"):
+    for name in ("a_kp", "a_km", "a_hr"):
         PE.wait_ge(S[name], 4)
     PE.wait_ge(S.q_e, 1)
     PE.wait_ge(S.r_ka, 2 * kn)
-    mm(bank(4, 512), kblk(0), es(0, 512), S.m_z0)
-    mm(bank(5, 512), kblk(2), es(0, 512), S.m_z2)
-    PE.wait_ge(S.r_kb, kn)
-    mm(bank(6, 512), kblk(1), es(0, 512), S.m_z1)
-    mm(bank(7, 256), kblk(3), es(0, 256), S.m_z3a)
-    mm(bank(0, 256), kblk(3), es(256, 512), S.m_z3b)
+    zmm(0, 6, 7)
+    zmm(2, 4, 5)
+    PE.wait_ge(S.r_k1, 2 * kn)
+    zmm(1, 0, 3)
+    PE.wait_ge(S.c_z0, 2)
+    PE.wait_ge(S.r_k3, kn)
+    zmm(3, 6, 7)
     PE.wait_ge(S.q_w2, 1)
-    PE.wait_ge(S.r_h, 3 * hn)
-    v = (T.qv[:, 0:128], T.sv[:, 0:128])
-    mm(bank(1, 256), v, (T.rh[:, 0:256], T.rsh[:, 0:256]), S.m_ya)
-    mm(bank(2, 256), v, (T.rh[:, 256:512], T.rsh[:, 256:512]), S.m_yb)
+    v = pair(T.qv, T.sv, 0, 128)
+    PE.wait_ge(S.r_hh, (len(PIECES) + 1) * hh)
+    mm(bank(1, HT), v, pair(T.rh, T.rsh, 0, HT), S.m_ya)
+    PE.wait_ge(S.r_hr, 2 * hr)
+    mm(bank(2, 512 - HT), v, pair(T.rh, T.rsh, HT, 512), S.m_yb)
 
     def copy_v(dst, i, w, done, sem):
         V.wait_ge(done, 1)
@@ -185,23 +224,18 @@ def rank_program(g, core, T, topo):
         A.wait_ge(done, 1)
         A.activation(dst, bank(i, w), COPY).then_inc(sem, 1)
 
-    copy_v(T.zo[:, 0:512], 4, 512, S.m_z0, S.c_z0)
-    copy_s(T.zo[:, 1024:1536], 5, 512, S.m_z2, S.c_z2)
-    copy_v(T.zo[:, 512:1024], 6, 512, S.m_z1, S.c_z1)
-    copy_s(T.zo[:, 1536:1792], 7, 256, S.m_z3a, S.c_z3)
-    copy_v(T.zo[:, 1792:2048], 0, 256, S.m_z3b, S.c_z3)
+    for b, i, j in ((0, 6, 7), (2, 4, 5), (1, 0, 3), (3, 6, 7)):
+        copy_s(T.zo[:, 512 * b:512 * b + 256], i, 256, S["m_z%da" % b], S["c_z%d" % b])
+        copy_v(T.zo[:, 512 * b + 256:512 * b + 512], j, 256, S["m_z%db" % b], S["c_z%d" % b])
     A.wait_ge(S.c_z3, 2)
     A.dma_start(T.z[:, 1536:2048], T.zo[:, 1536:2048]).then_inc(S.st_a, 16)
-    copy_s(T.yo[:, 0:256], 1, 256, S.m_ya, S.c_y)
-    copy_v(T.yo[:, 256:512], 2, 256, S.m_yb, S.c_y)
+    copy_s(T.yo[:, 0:HT], 1, HT, S.m_ya, S.c_y)
+    copy_v(T.yo[:, HT:512], 2, 512 - HT, S.m_yb, S.c_y)
     A.wait_ge(S.st_a, 16)
 
-    SY.wait_ge(S.c_z0, 1)
-    SY.dma_start(T.z[:, 0:512], T.zo[:, 0:512]).then_inc(S.st_s, 16)
-    SY.wait_ge(S.c_z2, 1)
-    SY.dma_start(T.z[:, 1024:1536], T.zo[:, 1024:1536]).then_inc(S.st_s, 16)
-    SY.wait_ge(S.c_z1, 1)
-    SY.dma_start(T.z[:, 512:1024], T.zo[:, 512:1024]).then_inc(S.st_s, 16)
+    for b in (0, 2, 1):
+        SY.wait_ge(S["c_z%d" % b], 2)
+        SY.dma_start(T.z[:, 512 * b:512 * b + 512], T.zo[:, 512 * b:512 * b + 512]).then_inc(S.st_s, 16)
     SY.wait_ge(S.c_y, 2)
     SY.dma_start(T.y[:], T.yo[:]).then_inc(S.st_s, 16)
     SY.wait_ge(S.st_s, 64)

from concourse.mybir import dt, AluOpType, ActivationFunctionType

C = 0.043
CORES_SIMULATED = 96
XP = [(0, 128), (128, 384), (384, 512)]
HT = 320
PIECES = [(0, 128), (128, HT)]

Q, U, B, F = "float8_e4m3fn_x4", "uint8", "bfloat16", "float32"
SCRATCH = {"ps": ("psum", [128, 4096], F)}
for _name, _cols, _dtype in (
        ("xb", 2048, B), ("wb", 1024, B), ("w2b", 512, B), ("eb", 2048, B),
        ("qx", 512, Q), ("sx", 512, U), ("qw", 256, Q), ("sw", 256, U),
        ("qv", 128, Q), ("sv", 128, U), ("qe", 512, Q), ("se", 512, U),
        ("kb", 2048, B), ("qk", 512, Q), ("sk", 512, U),
        ("hb", 2048, B), ("qh", 512, Q), ("sh", 512, U),
        ("rk", 512, Q), ("rsk", 512, U), ("rh", 512, Q), ("rsh", 512, U),
        ("yo", 512, F), ("zo", 2048, F)):
    SCRATCH[_name] = ("sbuf", [128, _cols], _dtype)
SEMAPHORES = (
    "l_x0 l_x1 l_x2 l_w l_w2 l_e q_x0 q_x1 q_x2 q_x3 q_w q_w2 q_e "
    "m_k0 m_k1 m_k2 m_k3 a_kp a_km q_kp q_km "
    "m_ra m_rb a_hr q_hr "
    "r_w r_x m_a0 m_a1 m_b0 m_b1 a_h0 a_h1 q_h0 q_h1 "
    "sent r_ka r_k1 r_k3 r_hh r_hr "
    "m_z0a m_z0b m_z1a m_z1b m_z2a m_z2b m_z3a m_z3b m_ya m_yb "
    "c_z0 c_z1 c_z2 c_z3 c_y st_s st_a").split()


def engines(mask):
    return bin(mask).count("1")


def rank_program(g, core, T, topo):
    n = len(T.cores)
    S = T.sem
    V, A, PE, SY = g.vector, g.scalar, g.tensor, g.sync
    MULT, MAX = AluOpType.mult, AluOpType.max
    RELU, COPY = ActivationFunctionType.Relu, ActivationFunctionType.Copy

    def helper_of(r):
        c = T.cores[r]
        return [d for d in range(CORES_SIMULATED) if topo.chip(d) == topo.chip(c) and topo.die(d) != topo.die(c)
                and topo.may_write(d, T.cores[(r + 1) % n])][0]

    helpers = [helper_of(r) for r in range(n)]
    rank = T.rank_of(core)
    if rank is None and core not in helpers:
        return

    def bank(i, w):
        return T.ps[:, 512 * i:512 * i + w]

    def act_s(out, i, w, c, sem):
        A.activation(out, bank(i, w), RELU, bias=0.0, scale=c).then_inc(sem, 1)

    def act_v(out, i, w, c, sem):
        V.tensor_scalar(out, bank(i, w), c, 0.0, MULT, MAX).then_inc(sem, 1)

    def quant(q, s, b, lo, hi, sem):
        V.quantize_mx(q[:, lo:hi], s[:, lo:hi], b[:, 4 * lo:4 * hi]).then_inc(sem, 1)

    def mm(out, w, x, sem):
        PE.matmul_mx(out, w[0], w[1], x[0], x[1], True, True).then_inc(sem, 1)

    def pair(q, s, lo, hi):
        return q[:, lo:hi], s[:, lo:hi]

    def write(dst, out, src, sem):
        rid, pid, _ = topo.addr(dst)
        g.remote_dma(out, src, sem, S.sent, pid, rid, topo.mask(core, dst))
        return engines(topo.mask(core, dst))

    def put_codes(dst, out, src, lo, hi, sem):
        return write(dst, out[:, lo:hi].bitcast(dt.uint8), src[:, lo:hi].bitcast(dt.uint8), sem)

    def put_plane(dst, out, src, lo, hi, sem):
        return write(dst, out[:, lo:hi], src[:, lo:hi], sem)

    def hcols(b, lo, hi):
        return T.hb[:, 4 * lo + b:4 * hi:4]

    if rank is None:
        r = helpers.index(core)
        dst = T.cores[(r + 1) % n]
        on = engines(topo.mask(T.cores[r], core))
        PE.wait_ge(S.r_w, 4 * on)
        out = 0
        for i, (lo, hi) in enumerate(PIECES):
            if i == 1:
                PE.wait_ge(S.r_x, 2 * on)
            mm(bank(2 * i, hi - lo), pair(T.qw, T.sw, 0, 128), pair(T.qx, T.sx, lo, hi), S["m_a%d" % i])
            mm(bank(2 * i + 1, hi - lo), pair(T.qw, T.sw, 128, 256), pair(T.qx, T.sx, lo, hi), S["m_b%d" % i])
            done = S["a_h%d" % i]
            A.wait_ge(S["m_a%d" % i], 1)
            act_s(hcols(0, lo, hi), 2 * i, hi - lo, C, done)
            act_s(hcols(1, lo, hi), 2 * i, hi - lo, -C, done)
            V.wait_ge(S["m_b%d" % i], 1)
            act_v(hcols(2, lo, hi), 2 * i + 1, hi - lo, C, done)
            act_v(hcols(3, lo, hi), 2 * i + 1, hi - lo, -C, done)
            V.wait_ge(done, 4)
            quant(T.qh, T.sh, T.hb, lo, hi, S["q_h%d" % i])
            g.wait_ge(S["q_h%d" % i], 1)
            if i == 1:
                out += put_plane(dst, T.rsh, T.sh, 0, HT, S.r_hh)
            out += put_codes(dst, T.rh, T.qh, lo, hi, S.r_hh)
        g.wait_ge(S.sent, out)
        return

    helper, prev, nxt = helpers[rank], T.cores[(rank - 1) % n], T.cores[(rank + 1) % n]

    def kcols(s, t):
        return T.kb[:, 1024 * s + t:1024 * s + 1024:4]

    def load_x(i):
        lo, hi = XP[i]
        SY.dma_start(T.xb[:, 4 * lo:4 * hi], T.x[:, 4 * lo:4 * hi]).then_inc(S["l_x%d" % i], 16)

    load_x(0)
    SY.dma_start(T.wb[:], T.w1[:]).then_inc(S.l_w, 16)
    load_x(1)
    load_x(2)
    SY.dma_start(T.eb[:], T.e[:]).then_inc(S.l_e, 16)
    SY.wait_ge(S.q_kp, 1)
    SY.dma_start(T.w2b[:], T.w2[:]).then_inc(S.l_w2, 16)

    PE.wait_ge(S.q_w, 1)
    for t in range(4):
        PE.wait_ge(S["q_x%d" % t], 1)
        mm(bank(t, 256), pair(T.qx, T.sx, 128 * t, 128 * t + 128), pair(T.qw, T.sw, 0, 256), S["m_k%d" % t])
    mm(bank(4, 512 - HT), pair(T.qw, T.sw, 0, 128), pair(T.qx, T.sx, HT, 512), S.m_ra)
    mm(bank(5, 512 - HT), pair(T.qw, T.sw, 128, 256), pair(T.qx, T.sx, HT, 512), S.m_rb)

    for t in (0, 1, 3):
        A.wait_ge(S["m_k%d" % t], 1)
        act_s(kcols(0, t), t, 256, C, S.a_kp)
    for t in (0, 1, 3):
        act_s(kcols(1, t), t, 256, -C, S.a_km)
    A.wait_ge(S.m_ra, 1)
    act_s(hcols(0, HT, 512), 4, 512 - HT, C, S.a_hr)
    act_s(hcols(1, HT, 512), 4, 512 - HT, -C, S.a_hr)

    V.wait_ge(S.l_x0, 16)
    quant(T.qx, T.sx, T.xb, 0, 128, S.q_x0)
    V.wait_ge(S.l_w, 16)
    quant(T.qw, T.sw, T.wb, 0, 256, S.q_w)
    V.wait_ge(S.l_x1, 16)
    quant(T.qx, T.sx, T.xb, 128, 256, S.q_x1)
    quant(T.qx, T.sx, T.xb, 256, 384, S.q_x2)
    V.wait_ge(S.l_x2, 16)
    quant(T.qx, T.sx, T.xb, 384, 512, S.q_x3)
    V.wait_ge(S.m_k2, 1)
    act_v(kcols(0, 2), 2, 256, C, S.a_kp)
    V.wait_ge(S.a_kp, 4)
    quant(T.qk, T.sk, T.kb, 0, 256, S.q_kp)
    act_v(kcols(1, 2), 2, 256, -C, S.a_km)
    V.wait_ge(S.a_km, 4)
    quant(T.qk, T.sk, T.kb, 256, 512, S.q_km)
    V.wait_ge(S.m_rb, 1)
    act_v(hcols(2, HT, 512), 5, 512 - HT, C, S.a_hr)
    act_v(hcols(3, HT, 512), 5, 512 - HT, -C, S.a_hr)
    V.wait_ge(S.a_hr, 4)
    quant(T.qh, T.sh, T.hb, HT, 512, S.q_hr)
    V.wait_ge(S.l_e, 16)
    quant(T.qe, T.se, T.eb, 0, 512, S.q_e)
    V.wait_ge(S.l_w2, 16)
    quant(T.qv, T.sv, T.w2b, 0, 128, S.q_w2)

    g.wait_ge(S.q_x0, 1)
    out = put_codes(helper, T.qx, T.qx, 0, 128, S.r_w)
    g.wait_ge(S.q_w, 1)
    out += put_codes(helper, T.qw, T.qw, 0, 256, S.r_w)
    out += put_plane(helper, T.sx, T.sx, 0, 128, S.r_w)
    out += put_plane(helper, T.sw, T.sw, 0, 256, S.r_w)
    for t in (1, 2):
        g.wait_ge(S["q_x%d" % t], 1)
    out += put_plane(helper, T.sx, T.sx, 128, HT, S.r_x)
    out += put_codes(helper, T.qx, T.qx, 128, HT, S.r_x)
    g.wait_ge(S.q_kp, 1)
    out += put_codes(prev, T.rk, T.qk, 0, 256, S.r_ka)
    out += put_plane(prev, T.rsk, T.sk, 0, 256, S.r_ka)
    g.wait_ge(S.q_km, 1)
    out += put_plane(prev, T.rsk, T.sk, 256, 512, S.r_k1)
    out += put_codes(prev, T.rk, T.qk, 256, 384, S.r_k1)
    out += put_codes(prev, T.rk, T.qk, 384, 512, S.r_k3)
    g.wait_ge(S.q_hr, 1)
    out += put_plane(nxt, T.rsh, T.sh, HT, 512, S.r_hr)
    out += put_codes(nxt, T.rh, T.qh, HT, 512, S.r_hr)
    g.wait_ge(S.sent, out)

    kn = engines(topo.mask(nxt, core))
    hh = engines(topo.mask(helpers[(rank - 1) % n], core))
    hr = engines(topo.mask(prev, core))

    def zmm(b, i, j):
        lo = 256 * (b % 2) + 128 * (b // 2)
        k = pair(T.rk, T.rsk, lo, lo + 128)
        mm(bank(i, 256), k, pair(T.qe, T.se, 0, 256), S["m_z%da" % b])
        mm(bank(j, 256), k, pair(T.qe, T.se, 256, 512), S["m_z%db" % b])

    for name in ("a_kp", "a_km", "a_hr"):
        PE.wait_ge(S[name], 4)
    PE.wait_ge(S.q_e, 1)
    PE.wait_ge(S.r_ka, 2 * kn)
    zmm(0, 6, 7)
    zmm(2, 4, 5)
    PE.wait_ge(S.r_k1, 2 * kn)
    zmm(1, 0, 3)
    PE.wait_ge(S.c_z0, 2)
    PE.wait_ge(S.r_k3, kn)
    zmm(3, 6, 7)
    PE.wait_ge(S.q_w2, 1)
    v = pair(T.qv, T.sv, 0, 128)
    PE.wait_ge(S.r_hh, (len(PIECES) + 1) * hh)
    mm(bank(1, HT), v, pair(T.rh, T.rsh, 0, HT), S.m_ya)
    PE.wait_ge(S.r_hr, 2 * hr)
    mm(bank(2, 512 - HT), v, pair(T.rh, T.rsh, HT, 512), S.m_yb)

    def copy_v(dst, i, w, done, sem):
        V.wait_ge(done, 1)
        V.tensor_copy(dst, bank(i, w)).then_inc(sem, 1)

    def copy_s(dst, i, w, done, sem):
        A.wait_ge(done, 1)
        A.activation(dst, bank(i, w), COPY).then_inc(sem, 1)

    for b, i, j in ((0, 6, 7), (2, 4, 5), (1, 0, 3), (3, 6, 7)):
        copy_s(T.zo[:, 512 * b:512 * b + 256], i, 256, S["m_z%da" % b], S["c_z%d" % b])
        copy_v(T.zo[:, 512 * b + 256:512 * b + 512], j, 256, S["m_z%db" % b], S["c_z%d" % b])
    A.wait_ge(S.c_z3, 2)
    A.dma_start(T.z[:, 1536:2048], T.zo[:, 1536:2048]).then_inc(S.st_a, 16)
    copy_s(T.yo[:, 0:HT], 1, HT, S.m_ya, S.c_y)
    copy_v(T.yo[:, HT:512], 2, 512 - HT, S.m_yb, S.c_y)
    A.wait_ge(S.st_a, 16)

    for b in (0, 2, 1):
        SY.wait_ge(S["c_z%d" % b], 2)
        SY.dma_start(T.z[:, 512 * b:512 * b + 512], T.zo[:, 512 * b:512 * b + 512]).then_inc(S.st_s, 16)
    SY.wait_ge(S.c_y, 2)
    SY.dma_start(T.y[:], T.yo[:]).then_inc(S.st_s, 16)
    SY.wait_ge(S.st_s, 64)
